import numpy as np
import ml_dtypes


def mxq(x, axis, fmt="e4m3"):
    dtype, down = {"e4m3": (ml_dtypes.float8_e4m3fn, 7), "e5m2": (ml_dtypes.float8_e5m2, 14)}[fmt]
    v = np.moveaxis(np.asarray(x, np.float32).astype(ml_dtypes.bfloat16).astype(np.float64), axis, -1)
    blocks = v.reshape(v.shape[:-1] + (-1, 32))
    amax = np.abs(blocks).max(-1, keepdims=True)
    byte = np.maximum(np.where(amax > 0, np.frexp(amax)[1] - 1 + 127, 0) - down, 1)
    scale = np.exp2(byte - 127.0)
    codes = (blocks / scale).astype(np.float32).astype(dtype).astype(np.float64)
    return np.moveaxis((codes * scale).reshape(v.shape), -1, axis)


WIDE = False


def mx_kscale(k):
    if not WIDE:
        return np.ones(k)
    levels = np.array([10, -10, 5, -5, 0])
    if k % 512:
        return np.exp2(np.random.permutation(np.resize(levels, k // 32))).repeat(32)
    a = np.empty((k // 512, 16))
    for p in range(k // 512):
        a[p, :8] = np.random.permutation(np.resize(levels, 8))
        for g in range(8):
            far = levels[np.abs(levels - a[p, g]) >= 10]
            a[p, g + 8] = far[np.random.randint(len(far))]
    return np.exp2(a.ravel()).repeat(32)


def f64(x):
    return np.asarray(x).astype(np.float64)


def striped(idx):
    return np.tile(idx.reshape(-1, 16).T, (8, 1)).astype(np.uint16)


def unstriped(offs):
    return offs[:16].T.reshape(-1).astype(np.int64)


def sigmoid(v):
    return 1.0 / (1.0 + np.exp(-np.maximum(v, -700.0)))


K, T, E, C, H, N = 1024, 512, 4, 256, 512, 256


def by_expert(wq, xq):
    return np.concatenate([wq[e].T @ xq[:, e * C:(e + 1) * C] for e in range(E)], axis=1)


def setup_inputs():
    n = np.random.standard_normal
    s = mx_kscale(K)[:, None]
    u = mx_kscale(H)
    first = np.random.permutation(np.repeat(np.arange(E), T // E))
    second = (first + 1 + np.random.permutation(np.repeat(np.arange(E - 1), -(-T // (E - 1)))[:T])) % E
    while np.bincount(second, minlength=E).max() != T // E:
        load = np.bincount(second, minlength=E); hi, lo = int(load.argmax()), int(load.argmin())
        t = np.flatnonzero((second == hi) & (first != lo))[0]; second[t] = lo
    slot_token = np.empty(E * C, np.int64); pos = np.empty((2, T), np.int64); fill = np.zeros(E, np.int64)
    place = np.stack([np.random.permutation(C) for _ in range(E)])
    for r, deal in enumerate((first, second)):
        for t in np.random.permutation(T):
            e = deal[t]; j = e * C + place[e, fill[e]]; fill[e] += 1; slot_token[j] = t; pos[r, t] = j
    g = np.random.uniform(0.2, 0.8, T)
    return {
        "xT": (n((K, T)) * s).astype(np.float32),
        "w1": (n((E + 1, K, H)) / np.sqrt(K) / s[None]).astype(np.float32),
        "w3": (n((E + 1, K, H)) / np.sqrt(K) / s[None] * u[None, None, :]).astype(np.float32),
        "w2": (n((E + 1, H, N)) / np.sqrt(H) / u[None, :, None]).astype(np.float32),
        "gate": np.stack([np.tile(g, (N, 1)), np.tile(1.0 - g, (N, 1))]).astype(np.float32),
        "offs": striped(slot_token),
        "pos1": striped(pos[0]),
        "pos2": striped(pos[1]),
    }


def reference(xT, w1, w3, w2, gate, offs, pos1, pos2):
    idx = unstriped(offs)
    w1q, w3q, w2q = mxq(f64(w1), 1, "e4m3"), mxq(f64(w3), 1, "e4m3"), mxq(f64(w2), 1, "e4m3")
    xs = mxq(f64(xT), 0, "e4m3")
    hs = sigmoid(w1q[E].T @ xs) * (w3q[E].T @ xs)
    ys = w2q[E].T @ mxq(hs, 0, "e4m3")
    xq = mxq(f64(xT)[:, idx], 0, "e4m3")
    h = sigmoid(by_expert(w1q, xq))
    h = h * by_expert(w3q, xq)
    y = by_expert(w2q, mxq(h, 0, "e4m3"))
    return ys + f64(gate[0]) * y[:, unstriped(pos1)] + f64(gate[1]) * y[:, unstriped(pos2)]

@@ -1,0 +1,276 @@
+from contextlib import ExitStack
+
+import concourse.mybir as mybir
+
+FLOPS = 3623878656
+
+K, T, E, C, H, N = 1024, 512, 4, 256, 512, 256
+P = 128
+PACK = 4
+K_PASS = P * PACK
+PASSES = K // K_PASS
+GROUP = 128
+RING = 3
+W2_ENGINE = "SVSV"
+
+F32 = mybir.dt.float32
+BF16 = mybir.dt.bfloat16
+U32 = mybir.dt.uint32
+U16 = mybir.dt.uint16
+U8 = mybir.dt.uint8
+FP8X4 = mybir.dt.float8_e4m3fn_x4
+mult = mybir.AluOpType.mult
+add = mybir.AluOpType.add
+Sigmoid = mybir.ActivationFunctionType.Sigmoid
+
+
+def tile_moe_shr_glu_sigmoid_kernel(tc, xT, w1, w3, w2, gate, offs, pos1, pos2, out):
+    nc = tc.nc
+    with ExitStack() as ctx:
+        keep = ctx.enter_context(tc.tile_pool(name="keep", bufs=1))
+        pool = ctx.enter_context(tc.tile_pool(name="pool", bufs=1))
+        psum = ctx.enter_context(tc.psum_pool(name="psum", bufs=3))
+
+        offs_sb = keep.tile([P, E * C // 16], U16, name="offs_sb")
+        pos1_sb = keep.tile([P, T // 16], U16, name="pos1_sb")
+        pos2_sb = keep.tile([P, T // 16], U16, name="pos2_sb")
+
+        dummy = keep.tile([P, 1], F32, name="dummy")
+        nc.vector.memset(dummy[:], 0.0)
+        nc.scalar.activation(dummy[:], dummy[:], Sigmoid)
+
+        def load_raw(rows):
+            raw = pool.tile([P, PACK, 512], F32, name="raw", bufs=8)
+            nc.sync.dma_start(raw[:], rows.rearrange("(p j) w -> p j w", j=PACK))
+            return raw
+
+        def load_w2(e):
+            raw2 = pool.tile([P, PACK, N], F32, name="raw2", bufs=2)
+            nc.sync.dma_start(raw2[:], w2[e].rearrange("(p j) w -> p j w", j=PACK))
+            return raw2
+
+        def k_rows(c):
+            return slice(c * K_PASS, (c + 1) * K_PASS)
+
+        def quantize(grouped, width, name, bufs):
+            codes = pool.tile([P, width], U32, name=name + "_codes", bufs=bufs, align_bytes=64)
+            scales = pool.tile([P, width], U8, name=name + "_scales", bufs=bufs, align_bytes=64)
+            nc.vector.quantize_mx(out=codes[:].bitcast(FP8X4), scales=scales[:], in_=grouped)
+            return codes, scales
+
+        def copy(engine, dst, src):
+            if engine == "S":
+                nc.scalar.copy(dst, src)
+            else:
+                nc.vector.tensor_copy(dst, src)
+
+        ring = [keep.tile([P, H * PACK], BF16, name="ring%d" % i, align_bytes=64) for i in range(RING)]
+        turns = [0]
+
+        def next_ring(width):
+            grouped = ring[turns[0] % RING]
+            turns[0] += 1
+            return grouped[:, :width]
+
+        def group_w13(raw, engine):
+            grouped = next_ring(H * PACK)
+            copy(
+                engine,
+                grouped.rearrange("p (t m j) -> p m j t", t=PACK, j=PACK),
+                raw[:].rearrange("p j (m t) -> p m j t", t=PACK),
+            )
+            return grouped
+
+        def group_w2(raw2, engine):
+            grouped = next_ring(N * PACK)
+            copy(
+                engine,
+                grouped.rearrange("p (c i j) -> p c j i", i=4, j=PACK),
+                raw2[:].rearrange("p j (c i) -> p c j i", i=4),
+            )
+            return grouped
+
+        nc.sync.dma_start(offs_sb[:], offs)
+        x_raw = [load_raw(xT[k_rows(c), :]) for c in range(PASSES)]
+
+        def load_w13(w, e):
+            return [load_raw(w[e][k_rows(c), :]) for c in range(PASSES)]
+
+        x_pairs = []
+        for c in range(PASSES):
+            pairs = keep.tile([P, 2 * T * 2], BF16, name="pairs%d" % c, align_bytes=64)
+            for u in range(2):
+                copy(
+                    ("SV", "SS")[c][u],
+                    pairs[:, u * 2 * T : (u + 1) * 2 * T].rearrange("p (c i e) -> p c e i", i=4, e=2),
+                    x_raw[c][:, 2 * u : 2 * u + 2, :].rearrange("p e (c i) -> p c e i", i=4),
+                )
+            x_pairs.append(pairs)
+
+        def mx(acc, lhs, cols, rhs, slots, start, stop):
+            nc.tensor.matmul_mx(
+                out=acc,
+                lhsT=lhs[0][:, cols].bitcast(FP8X4),
+                lhsT_scale=lhs[1][:, cols],
+                rhs=rhs[0][:, slots].bitcast(FP8X4),
+                rhs_scale=rhs[1][:, slots],
+                start=start,
+                stop=stop,
+            )
+
+        def first_layer(name, wq, xq, g):
+            bank = psum.tile([P, PACK, GROUP], F32, name=name, bufs=3)
+            for t in range(PACK):
+                for c in range(PASSES):
+                    mx(bank[:, t, :], wq[c], slice(t * P, (t + 1) * P), xq[c], slice(g * GROUP, (g + 1) * GROUP), c == 0, c == PASSES - 1)
+            return bank
+
+        def second_layer(w2q, hq):
+            y = psum.tile([P, 2, C], F32, name="bank_y", bufs=2)
+            for m in range(2):
+                mx(y[:, m, :], w2q, slice(m * P, (m + 1) * P), hq, slice(0, C), True, True)
+            return y
+
+        def quantize_h(h):
+            codes = pool.tile([P, C], U32, name="h_codes", bufs=2, align_bytes=64)
+            scales = pool.tile([P, C], U8, name="h_scales", bufs=2, align_bytes=64)
+            nc.vector.quantize_mx(out=codes[:].bitcast(FP8X4), scales=scales[:], in_=h[:].rearrange("p s t -> p (s t)"))
+            return codes, scales
+
+        y_slots = [keep.tile([P, E * C], F32, name="y_slots%d" % m) for m in range(2)]
+
+
+        def mults(h, banks, sigs):
+            for n in range(len(banks)):
+                nc.vector.tensor_tensor(h[:, n * GROUP : (n + 1) * GROUP, :], banks[n][:].rearrange("p t s -> p s t"), sigs[n][:], mult)
+
+        def sigmoids(banks):
+            sigs = []
+            for bank in banks:
+                sig = pool.tile([P, GROUP, PACK], F32, name="sig", bufs=5)
+                nc.scalar.activation(sig[:], bank[:].rearrange("p t s -> p s t"), Sigmoid)
+                sigs.append(sig)
+            return sigs
+
+        def load_expert(e):
+            return load_w13(w1, e), load_w13(w3, e), load_w2(e)
+
+        def gather_pass(xg, e, c):
+            words = xg[:, c * C * PACK : (c + 1) * C * PACK].bitcast(U32).rearrange("p (s u) -> p s u", u=2)
+            for u in (1, 0):
+                window = x_pairs[c][:, u * 2 * T : (u + 1) * 2 * T].bitcast(U32)
+                nc.vector.tensor_copy(words[:, :, u], window.indirect(offs_sb[:, e * C // 16 : (e + 1) * C // 16]))
+
+        def shared_pass(xs, c):
+            nc.vector.tensor_copy(
+                xs[:, c * T * PACK : (c + 1) * T * PACK].rearrange("p (t u e) -> p t u e", u=2, e=2),
+                x_pairs[c][:].rearrange("p (u t e) -> p t u e", u=2, e=2),
+            )
+
+        def new_x(e):
+            if e < E:
+                xg = pool.tile([P, PASSES * C * PACK], BF16, name="xg", bufs=2, align_bytes=64)
+            else:
+                xg = keep.tile([P, PASSES * T * PACK], BF16, name="xs", align_bytes=64)
+            return xg
+
+        def fill_x(xg, e, c):
+            if e < E:
+                gather_pass(xg, e, c)
+            else:
+                shared_pass(xg, c)
+
+        def quantize_tokens(xg, e):
+            n = C if e < E else T
+            codes, scales = quantize(xg[:], PASSES * n, "xq" if e < E else "xsq", 2 if e < E else 1)
+            return [(codes[:, c * n : (c + 1) * n], scales[:, c * n : (c + 1) * n]) for c in range(PASSES)]
+
+        def finish_expert(done):
+            h, banks, sigs, w2g = done
+            mults(h, banks, sigs)
+            w2q = quantize(w2g, N, "w2q", 2)
+            hq = quantize_h(h)
+            return second_layer(w2q, hq)
+
+        def copy_y(y, e):
+            for m in range(2):
+                nc.scalar.copy(y_slots[m][:, e * C : (e + 1) * C], y[:, m, :])
+
+        raws = load_expert(0)
+        xg = new_x(0)
+        for c in range(PASSES):
+            fill_x(xg, 0, c)
+        xq = quantize_tokens(xg, 0)
+        done = None
+        for e in range(E):
+            r1, r3, r2 = raws
+            g0 = group_w13(r1[0], "S")
+            if e == E - 1:
+                nc.sync.dma_start(pos1_sb[:], pos1)
+                nc.sync.dma_start(pos2_sb[:], pos2)
+                gates = [keep.tile([P, 2, T], F32, name="gate%d" % r) for r in range(2)]
+                for r in range(2):
+                    nc.sync.dma_start(gates[r][:], gate[r].rearrange("(m p) t -> p m t", p=P))
+                s1 = load_w13(w1, E)
+                s2 = load_w2(E)
+                s3 = load_w13(w3, E)
+                raws = s1, s3, s2
+            else:
+                raws = load_expert(e + 1)
+            if done:
+                y = finish_expert(done)
+            xg = new_x(e + 1)
+            fill_x(xg, e + 1, 0)
+            g1 = group_w13(r1[1], "S")
+            if done:
+                copy_y(y, e - 1)
+            q0 = quantize(g0, H, "wq", 10)
+            fill_x(xg, e + 1, 1)
+            q1 = quantize(g1, H, "wq", 10)
+            banks_a = [first_layer("bank_a", (q0, q1), xq, g) for g in range(2)]
+            g0 = group_w13(r3[0], "S")
+            sigs = sigmoids(banks_a)
+            g1 = group_w13(r3[1], "V")
+            q0 = quantize(g0, H, "wq", 10)
+            new_xq = quantize_tokens(xg, e + 1)
+            q1 = quantize(g1, H, "wq", 10)
+            banks_b = [first_layer("bank_b", (q0, q1), xq, g) for g in range(2)]
+            w2g = group_w2(r2, W2_ENGINE[e])
+            h = pool.tile([P, C, PACK], BF16, name="h", bufs=3, align_bytes=64)
+            done = h, banks_b, sigs, w2g
+            xq = new_xq
+
+        r1, r3, r2 = raws
+        g0 = group_w13(r1[0], "S")
+        y = finish_expert(done)
+        g1 = group_w13(r1[1], "V")
+        copy_y(y, E - 1)
+        q0 = quantize(g0, H, "wq", 10)
+        q1 = quantize(g1, H, "wq", 10)
+        w2g = group_w2(r2, "V")
+        g0 = group_w13(r3[0], "S")
+        routed = [keep.tile([P, 2, T], F32, name="routed%d" % r) for r in range(2)]
+
+        def combine(r, m):
+            nc.vector.tensor_tensor(routed[r][:, m, :], y_slots[m][:].indirect((pos1_sb, pos2_sb)[r][:]), gates[r][:, m, :], mult)
+
+        combine(0, 0)
+        w2q = quantize(w2g, N, "w2q", 2)
+        combine(1, 0)
+        sigs = sigmoids([first_layer("bank_a", (q0, q1), xq, g) for g in range(4)])
+        q0 = quantize(g0, H, "wq", 10)
+        g1 = group_w13(r3[1], "V")
+        combine(0, 1)
+        q1 = quantize(g1, H, "wq", 10)
+        combine(1, 1)
+        both = keep.tile([P, 2, T], F32, name="both")
+        nc.vector.tensor_tensor(both[:], routed[0][:], routed[1][:], add)
+        for half in range(2):
+            h = pool.tile([P, C, PACK], BF16, name="h", bufs=3, align_bytes=64)
+            mults(h, [first_layer("bank_b", (q0, q1), xq, 2 * half + g) for g in range(2)], sigs[2 * half : 2 * half + 2])
+            hq = quantize_h(h)
+            y = second_layer(w2q, hq)
+            tokens = slice(half * C, (half + 1) * C)
+            result = pool.tile([P, 2, C], F32, name="result", bufs=2)
+            nc.vector.tensor_tensor(result[:], y[:], both[:, :, tokens], add)
+            nc.sync.dma_start(out[:, tokens].rearrange("(m p) t -> p m t", p=P), result[:])

@@ -10,267 +10,309 @@ PACK = 4
 K_PASS = P * PACK
 PASSES = K // K_PASS
 GROUP = 128
-RING = 3
-W2_ENGINE = "SVSV"
+LINE = 16
+
+SCALAR_SETS = {"w1": (128, 96), "w3": (0, 128), "w2": 32}
+SCALAR_SETS_SHARED = {"w1": (128, 96), "w3": (96, 128), "w2": 64}
 
 F32 = mybir.dt.float32
 BF16 = mybir.dt.bfloat16
+I32 = mybir.dt.int32
 U32 = mybir.dt.uint32
 U16 = mybir.dt.uint16
 U8 = mybir.dt.uint8
 FP8X4 = mybir.dt.float8_e4m3fn_x4
-mult = mybir.AluOpType.mult
-add = mybir.AluOpType.add
-Sigmoid = mybir.ActivationFunctionType.Sigmoid
+MULT = mybir.AluOpType.mult
+ADD = mybir.AluOpType.add
+SIGMOID = mybir.ActivationFunctionType.Sigmoid
 
 
-def tile_moe_shr_glu_sigmoid_kernel(tc, xT, w1, w3, w2, gate, offs, pos1, pos2, out):
+def tile_moe_shr_glu_sigmoid_kernel(
+    tc, xT, w1, w3, w2, gate, offs, pos1, pos2, out
+):
     nc = tc.nc
     with ExitStack() as ctx:
         keep = ctx.enter_context(tc.tile_pool(name="keep", bufs=1))
         pool = ctx.enter_context(tc.tile_pool(name="pool", bufs=1))
-        psum = ctx.enter_context(tc.psum_pool(name="psum", bufs=3))
+        psum = ctx.enter_context(tc.psum_pool(name="psum", bufs=1))
 
-        offs_sb = keep.tile([P, E * C // 16], U16, name="offs_sb")
-        pos1_sb = keep.tile([P, T // 16], U16, name="pos1_sb")
-        pos2_sb = keep.tile([P, T // 16], U16, name="pos2_sb")
+        offs_sb = keep.tile([P, E * C // LINE], U16, name="offs_sb")
+        pos_sb = [keep.tile([P, T // LINE], U16, name="pos_sb%d" % r) for r in range(2)]
+        gate_sb = [keep.tile([P, 2, T], F32, name="gate_sb%d" % r) for r in range(2)]
 
-        dummy = keep.tile([P, 1], F32, name="dummy")
-        nc.vector.memset(dummy[:], 0.0)
-        nc.scalar.activation(dummy[:], dummy[:], Sigmoid)
+        warm = keep.tile([P, 1], F32, name="warm")
+        nc.vector.memset(warm[:], 0.0)
+        nc.scalar.activation(warm[:], warm[:], SIGMOID)
 
-        def load_raw(rows):
-            raw = pool.tile([P, PACK, 512], F32, name="raw", bufs=8)
-            nc.sync.dma_start(raw[:], rows.rearrange("(p j) w -> p j w", j=PACK))
-            return raw
+        stages_w1 = [keep.tile([P, PASSES * H * PACK], BF16, name="stage_w1_%d" % i, align_bytes=64) for i in range(2)]
+        stage_w3 = keep.tile([P, PASSES * H * PACK], BF16, name="stage_w3", align_bytes=64)
+        stage_w2 = keep.tile([P, N * PACK], BF16, name="stage_w2", align_bytes=64)
 
-        def load_w2(e):
-            raw2 = pool.tile([P, PACK, N], F32, name="raw2", bufs=2)
-            nc.sync.dma_start(raw2[:], w2[e].rearrange("(p j) w -> p j w", j=PACK))
-            return raw2
-
-        def k_rows(c):
-            return slice(c * K_PASS, (c + 1) * K_PASS)
-
-        def quantize(grouped, width, name, bufs):
-            codes = pool.tile([P, width], U32, name=name + "_codes", bufs=bufs, align_bytes=64)
-            scales = pool.tile([P, width], U8, name=name + "_scales", bufs=bufs, align_bytes=64)
-            nc.vector.quantize_mx(out=codes[:].bitcast(FP8X4), scales=scales[:], in_=grouped)
-            return codes, scales
-
-        def copy(engine, dst, src):
-            if engine == "S":
-                nc.scalar.copy(dst, src)
-            else:
-                nc.vector.tensor_copy(dst, src)
-
-        ring = [keep.tile([P, H * PACK], BF16, name="ring%d" % i, align_bytes=64) for i in range(RING)]
-        turns = [0]
-
-        def next_ring(width):
-            grouped = ring[turns[0] % RING]
-            turns[0] += 1
-            return grouped[:, :width]
-
-        def group_w13(raw, engine):
-            grouped = next_ring(H * PACK)
-            copy(
-                engine,
-                grouped.rearrange("p (t m j) -> p m j t", t=PACK, j=PACK),
-                raw[:].rearrange("p j (m t) -> p m j t", t=PACK),
-            )
-            return grouped
-
-        def group_w2(raw2, engine):
-            grouped = next_ring(N * PACK)
-            copy(
-                engine,
-                grouped.rearrange("p (c i j) -> p c j i", i=4, j=PACK),
-                raw2[:].rearrange("p j (c i) -> p c j i", i=4),
-            )
-            return grouped
-
-        nc.sync.dma_start(offs_sb[:], offs)
-        x_raw = [load_raw(xT[k_rows(c), :]) for c in range(PASSES)]
-
-        def load_w13(w, e):
-            return [load_raw(w[e][k_rows(c), :]) for c in range(PASSES)]
-
-        x_pairs = []
-        for c in range(PASSES):
-            pairs = keep.tile([P, 2 * T * 2], BF16, name="pairs%d" % c, align_bytes=64)
-            for u in range(2):
-                copy(
-                    ("SV", "SS")[c][u],
-                    pairs[:, u * 2 * T : (u + 1) * 2 * T].rearrange("p (c i e) -> p c e i", i=4, e=2),
-                    x_raw[c][:, 2 * u : 2 * u + 2, :].rearrange("p e (c i) -> p c e i", i=4),
-                )
-            x_pairs.append(pairs)
-
-        def mx(acc, lhs, cols, rhs, slots, start, stop):
-            nc.tensor.matmul_mx(
-                out=acc,
-                lhsT=lhs[0][:, cols].bitcast(FP8X4),
-                lhsT_scale=lhs[1][:, cols],
-                rhs=rhs[0][:, slots].bitcast(FP8X4),
-                rhs_scale=rhs[1][:, slots],
-                start=start,
-                stop=stop,
-            )
-
-        def first_layer(name, wq, xq, g):
-            bank = psum.tile([P, PACK, GROUP], F32, name=name, bufs=3)
-            for t in range(PACK):
-                for c in range(PASSES):
-                    mx(bank[:, t, :], wq[c], slice(t * P, (t + 1) * P), xq[c], slice(g * GROUP, (g + 1) * GROUP), c == 0, c == PASSES - 1)
-            return bank
-
-        def second_layer(w2q, hq):
-            y = psum.tile([P, 2, C], F32, name="bank_y", bufs=2)
-            for m in range(2):
-                mx(y[:, m, :], w2q, slice(m * P, (m + 1) * P), hq, slice(0, C), True, True)
-            return y
-
-        def quantize_h(h):
-            codes = pool.tile([P, C], U32, name="h_codes", bufs=2, align_bytes=64)
-            scales = pool.tile([P, C], U8, name="h_scales", bufs=2, align_bytes=64)
-            nc.vector.quantize_mx(out=codes[:].bitcast(FP8X4), scales=scales[:], in_=h[:].rearrange("p s t -> p (s t)"))
-            return codes, scales
+        banks_a = [psum.tile([P, PACK, GROUP], F32, name="bank_a%d" % i) for i in range(4)]
+        banks_b = [psum.tile([P, PACK, GROUP], F32, name="bank_b%d" % i) for i in range(4)]
 
         y_slots = [keep.tile([P, E * C], F32, name="y_slots%d" % m) for m in range(2)]
 
 
-        def mults(h, banks, sigs):
-            for n in range(len(banks)):
-                nc.vector.tensor_tensor(h[:, n * GROUP : (n + 1) * GROUP, :], banks[n][:].rearrange("p t s -> p s t"), sigs[n][:], mult)
+        def four_rows(rows):
+            return rows.rearrange("(p j) w -> p j w", j=PACK)
 
-        def sigmoids(banks):
-            sigs = []
-            for bank in banks:
-                sig = pool.tile([P, GROUP, PACK], F32, name="sig", bufs=5)
-                nc.scalar.activation(sig[:], bank[:].rearrange("p t s -> p s t"), Sigmoid)
-                sigs.append(sig)
-            return sigs
+        def load_pass(rows):
+            raw = pool.tile([P, PACK, H], F32, name="raw", bufs=9)
+            nc.sync.dma_start(raw[:], four_rows(rows))
+            return raw
+
+        def load_w13(w, e, c):
+            return load_pass(w[e][c * K_PASS : (c + 1) * K_PASS, :])
+
+        def load_w2(e):
+            raw_w2 = pool.tile([P, PACK, N], F32, name="raw_w2", bufs=2)
+            nc.sync.dma_start(raw_w2[:], four_rows(w2[e]))
+            return raw_w2
 
         def load_expert(e):
-            return load_w13(w1, e), load_w13(w3, e), load_w2(e)
+            raw_w1 = [load_w13(w1, e, c) for c in range(PASSES)]
+            raw_w3 = [load_w13(w3, e, c) for c in range(PASSES)]
+            return raw_w1, raw_w3, load_w2(e)
 
-        def gather_pass(xg, e, c):
-            words = xg[:, c * C * PACK : (c + 1) * C * PACK].bitcast(U32).rearrange("p (s u) -> p s u", u=2)
-            for u in (1, 0):
-                window = x_pairs[c][:, u * 2 * T : (u + 1) * 2 * T].bitcast(U32)
-                nc.vector.tensor_copy(words[:, :, u], window.indirect(offs_sb[:, e * C // 16 : (e + 1) * C // 16]))
+        def load_gate(r):
+            nc.sync.dma_start(gate_sb[r][:], gate[r].rearrange("(m p) t -> p m t", p=P))
 
-        def shared_pass(xs, c):
-            nc.vector.tensor_copy(
-                xs[:, c * T * PACK : (c + 1) * T * PACK].rearrange("p (t u e) -> p t u e", u=2, e=2),
-                x_pairs[c][:].rearrange("p (u t e) -> p t u e", u=2, e=2),
+        def load_shared_expert():
+            raw_w1 = [load_w13(w1, E, c) for c in range(PASSES)]
+            nc.sync.dma_start(pos_sb[0][:], pos1)
+            nc.sync.dma_start(pos_sb[1][:], pos2)
+            load_gate(0)
+            raw_w3 = [load_w13(w3, E, c) for c in range(PASSES)]
+            raw_w2 = load_w2(E)
+            load_gate(1)
+            return raw_w1, raw_w3, raw_w2
+
+
+        def copy(engine, dst, src):
+            if engine == "scalar":
+                nc.scalar.copy(dst, src)
+            else:
+                nc.vector.tensor_copy(dst, src)
+
+        def split_copy(dst, src, scalar_sets, sets):
+            for engine, lo, hi in (("scalar", 0, scalar_sets), ("vector", scalar_sets, sets)):
+                if lo < hi:
+                    copy(engine, dst[:, lo:hi], src[:, lo:hi])
+
+        def half(stage, c):
+            return stage[:, c * H * PACK : (c + 1) * H * PACK]
+
+        def stage_w13(dst, raw, scalar_sets):
+            split_copy(
+                dst.rearrange("p (t m j) -> p m j t", t=PACK, j=PACK),
+                raw[:].rearrange("p j (m t) -> p m j t", t=PACK),
+                scalar_sets,
+                H // PACK,
             )
 
-        def new_x(e):
+        def stage_second(raw_w2, scalar_sets):
+            split_copy(
+                stage_w2[:].rearrange("p (m i j) -> p m j i", i=4, j=PACK),
+                raw_w2[:].rearrange("p j (m i) -> p m j i", i=4),
+                scalar_sets,
+                N // 4,
+            )
+
+        def quantize(staged, width, name, bufs):
+            codes = pool.tile([P, width], U32, name=name + "_codes", bufs=bufs, align_bytes=64)
+            scales = pool.tile([P, width], U8, name=name + "_scales", bufs=bufs, align_bytes=64)
+            nc.vector.quantize_mx(out=codes[:].bitcast(FP8X4), scales=scales[:], in_=staged)
+            return codes, scales
+
+        def quantize_w13(stage, c):
+            return quantize(half(stage, c), H, "wq", 8)
+
+        def quantize_w2():
+            return quantize(stage_w2[:], N, "w2q", 3)
+
+        def by_pass(operand, width):
+            codes, scales = operand
+            return [(codes[:, c * width : (c + 1) * width], scales[:, c * width : (c + 1) * width]) for c in range(PASSES)]
+
+
+        token_pairs = [keep.tile([P, 2 * T * 2], BF16, name="token_pairs%d" % c, align_bytes=64) for c in range(PASSES)]
+
+        def pair_plane(c, u):
+            return token_pairs[c][:, u * 2 * T : (u + 1) * 2 * T]
+
+        def load_tokens(c):
+            raw = pool.tile([P, PACK, T], F32, name="raw", bufs=9)
+            for u in (1, 0):
+                rows = slice(2 * u, 2 * u + 2)
+                nc.sync.dma_start(raw[:, rows, :], four_rows(xT[c * K_PASS : (c + 1) * K_PASS, :])[:, rows, :])
+            return raw
+
+        def pair_rows(raw, c, u, engine):
+            copy(
+                engine,
+                pair_plane(c, u).rearrange("p (m i e) -> p m e i", i=4, e=2),
+                raw[:, 2 * u : 2 * u + 2, :].rearrange("p e (m i) -> p m e i", i=4),
+            )
+
+        def stage_tokens(stage, e, c):
             if e < E:
-                xg = pool.tile([P, PASSES * C * PACK], BF16, name="xg", bufs=2, align_bytes=64)
+                lists = offs_sb[:, e * C // LINE : (e + 1) * C // LINE]
+                words = stage[:, (c + 1) * C * PACK : (c + 2) * C * PACK].bitcast(U32).rearrange("p (s u) -> p s u", u=2)
+                for u in (1, 0):
+                    nc.vector.tensor_copy(words[:, :, u], pair_plane(c, u).bitcast(U32).indirect(lists))
             else:
-                xg = keep.tile([P, PASSES * T * PACK], BF16, name="xs", align_bytes=64)
-            return xg
+                nc.vector.tensor_copy(
+                    half(stage, c).bitcast(I32).rearrange("p (s u) -> p s u", u=2),
+                    token_pairs[c][:].bitcast(I32).rearrange("p (u s) -> p s u", u=2),
+                )
 
-        def fill_x(xg, e, c):
+        def quantize_tokens(stage, e):
             if e < E:
-                gather_pass(xg, e, c)
-            else:
-                shared_pass(xg, c)
+                return by_pass(quantize(stage[:, C * PACK : (1 + PASSES) * C * PACK], PASSES * C, "xq", 2), C)
+            return by_pass(quantize(stage[:], PASSES * T, "xsq", 1), T)
 
-        def quantize_tokens(xg, e):
-            n = C if e < E else T
-            codes, scales = quantize(xg[:], PASSES * n, "xq" if e < E else "xsq", 2 if e < E else 1)
-            return [(codes[:, c * n : (c + 1) * n], scales[:, c * n : (c + 1) * n]) for c in range(PASSES)]
 
-        def finish_expert(done):
-            h, banks, sigs, w2g = done
-            mults(h, banks, sigs)
-            w2q = quantize(w2g, N, "w2q", 2)
-            hq = quantize_h(h)
-            return second_layer(w2q, hq)
+        def matmul_mx(acc, weights, weight_cols, moving, cols, start, stop):
+            nc.tensor.matmul_mx(
+                out=acc,
+                lhsT=weights[0][:, weight_cols].bitcast(FP8X4),
+                lhsT_scale=weights[1][:, weight_cols],
+                rhs=moving[0][:, cols].bitcast(FP8X4),
+                rhs_scale=moving[1][:, cols],
+                start=start,
+                stop=stop,
+            )
 
-        def copy_y(y, e):
+        def first_layer(bank, weights, tokens, g):
+            cols = slice(g * GROUP, (g + 1) * GROUP)
+            for t in range(PACK):
+                for c in range(PASSES):
+                    matmul_mx(
+                        bank[:, t, :], weights[c], slice(t * P, (t + 1) * P), tokens[c], cols, c == 0, c == PASSES - 1
+                    )
+
+        def sigmoid_of(bank, dst):
+            nc.scalar.activation(dst.rearrange("p (s t) -> p s t", t=PACK), bank[:].rearrange("p t s -> p s t"), SIGMOID)
+
+        def hidden(banks, sigmoids):
+            h = pool.tile([P, C, PACK], BF16, name="h", bufs=2, align_bytes=64)
+            for g in range(2):
+                nc.vector.tensor_tensor(
+                    h[:, g * GROUP : (g + 1) * GROUP, :],
+                    banks[g][:].rearrange("p t s -> p s t"),
+                    sigmoids[g].rearrange("p (s t) -> p s t", t=PACK),
+                    MULT,
+                )
+            return h
+
+        def quantize_hidden(h):
+            return quantize(h[:].rearrange("p s t -> p (s t)"), C, "hq", 3)
+
+        def second_layer(bank, weights, h):
+            y = bank[:].rearrange("p t s -> p (t s)").rearrange("p (m s) -> p m s", m=2)
             for m in range(2):
-                nc.scalar.copy(y_slots[m][:, e * C : (e + 1) * C], y[:, m, :])
+                matmul_mx(y[:, m, :], weights, slice(m * P, (m + 1) * P), h, slice(0, C), True, True)
+            return y
+
+        def keep_results(y, e, engine):
+            for m in range(2):
+                copy(engine, y_slots[m][:, e * C : (e + 1) * C], y[:, m, :])
+
+
+        nc.sync.dma_start(offs_sb[:], offs)
+        raw_tokens = [load_tokens(c) for c in range(PASSES)]
+        for c in range(PASSES):
+            for u in (1, 0):
+                pair_rows(raw_tokens[c], c, u, "scalar" if (c, u) == (1, 1) else "vector")
 
         raws = load_expert(0)
-        xg = new_x(0)
         for c in range(PASSES):
-            fill_x(xg, 0, c)
-        xq = quantize_tokens(xg, 0)
-        done = None
-        for e in range(E):
-            r1, r3, r2 = raws
-            g0 = group_w13(r1[0], "S")
-            if e == E - 1:
-                nc.sync.dma_start(pos1_sb[:], pos1)
-                nc.sync.dma_start(pos2_sb[:], pos2)
-                gates = [keep.tile([P, 2, T], F32, name="gate%d" % r) for r in range(2)]
-                for r in range(2):
-                    nc.sync.dma_start(gates[r][:], gate[r].rearrange("(m p) t -> p m t", p=P))
-                s1 = load_w13(w1, E)
-                s2 = load_w2(E)
-                s3 = load_w13(w3, E)
-                raws = s1, s3, s2
-            else:
-                raws = load_expert(e + 1)
-            if done:
-                y = finish_expert(done)
-            xg = new_x(e + 1)
-            fill_x(xg, e + 1, 0)
-            g1 = group_w13(r1[1], "S")
-            if done:
-                copy_y(y, e - 1)
-            q0 = quantize(g0, H, "wq", 10)
-            fill_x(xg, e + 1, 1)
-            q1 = quantize(g1, H, "wq", 10)
-            banks_a = [first_layer("bank_a", (q0, q1), xq, g) for g in range(2)]
-            g0 = group_w13(r3[0], "S")
-            sigs = sigmoids(banks_a)
-            g1 = group_w13(r3[1], "V")
-            q0 = quantize(g0, H, "wq", 10)
-            new_xq = quantize_tokens(xg, e + 1)
-            q1 = quantize(g1, H, "wq", 10)
-            banks_b = [first_layer("bank_b", (q0, q1), xq, g) for g in range(2)]
-            w2g = group_w2(r2, W2_ENGINE[e])
-            h = pool.tile([P, C, PACK], BF16, name="h", bufs=3, align_bytes=64)
-            done = h, banks_b, sigs, w2g
-            xq = new_xq
+            stage_tokens(stages_w1[1], 0, c)
+        tokens = quantize_tokens(stages_w1[1], 0)
 
-        r1, r3, r2 = raws
-        g0 = group_w13(r1[0], "S")
-        y = finish_expert(done)
-        g1 = group_w13(r1[1], "V")
-        copy_y(y, E - 1)
-        q0 = quantize(g0, H, "wq", 10)
-        q1 = quantize(g1, H, "wq", 10)
-        w2g = group_w2(r2, "V")
-        g0 = group_w13(r3[0], "S")
+        for e in range(E):
+            raw_w1, raw_w3, raw_w2 = raws
+            stage = stages_w1[e % 2]
+            stage_w13(half(stage, 0), raw_w1[0], SCALAR_SETS["w1"][0])
+            raws = load_expert(e + 1) if e + 1 < E else load_shared_expert()
+            if e > 0:
+                sigmoids = [raw_w1[0][:, g, :] for g in range(2)]
+                for g in range(2):
+                    sigmoid_of(a[g], sigmoids[g])
+                if e > 1:
+                    keep_results(second_layer(a[0], w2q, hq), e - 2, "scalar")
+                h = hidden(b, sigmoids)
+                w2q = quantize_w2()
+                hq = quantize_hidden(h)
+            w1q = [quantize_w13(stage, 0)]
+            stage_tokens(stage, e + 1, 0)
+            stage_w13(half(stage, 1), raw_w1[1], SCALAR_SETS["w1"][1])
+            w1q.append(quantize_w13(stage, 1))
+            stage_tokens(stage, e + 1, 1)
+            a = banks_a[2 * (e % 2) : 2 * (e % 2) + 2]
+            b = banks_b[2 * (e % 2) : 2 * (e % 2) + 2]
+            for g in range(2):
+                first_layer(a[g], w1q, tokens, g)
+            for c in range(PASSES):
+                stage_w13(half(stage_w3, c), raw_w3[c], SCALAR_SETS["w3"][c])
+            w3q = [quantize_w13(stage_w3, 0)]
+            next_tokens = quantize_tokens(stage, e + 1)
+            w3q.append(quantize_w13(stage_w3, 1))
+            for g in range(2):
+                first_layer(b[g], w3q, tokens, g)
+            stage_second(raw_w2, SCALAR_SETS["w2"])
+            tokens = next_tokens
+
+
+        raw_w1, raw_w3, raw_w2 = raws
+        stage = stages_w1[E % 2]
+        stage_w13(half(stage, 0), raw_w1[0], SCALAR_SETS_SHARED["w1"][0])
+        sigmoids = [raw_w1[0][:, g, :] for g in range(2)]
+        for g in range(2):
+            sigmoid_of(a[g], sigmoids[g])
+        keep_results(second_layer(a[0], w2q, hq), E - 2, "scalar")
+        h = hidden(b, sigmoids)
+        w2q = quantize_w2()
+        hq = quantize_hidden(h)
+        y = second_layer(banks_b[0], w2q, hq)
+        stage_w13(half(stage, 1), raw_w1[1], SCALAR_SETS_SHARED["w1"][1])
+        w1q = [quantize_w13(stage, 0)]
+        keep_results(y, E - 1, "vector")
+        w1q.append(quantize_w13(stage, 1))
+
+
         routed = [keep.tile([P, 2, T], F32, name="routed%d" % r) for r in range(2)]
 
         def combine(r, m):
-            nc.vector.tensor_tensor(routed[r][:, m, :], y_slots[m][:].indirect((pos1_sb, pos2_sb)[r][:]), gates[r][:, m, :], mult)
+            nc.vector.tensor_tensor(routed[r][:, m, :], y_slots[m][:].indirect(pos_sb[r][:]), gate_sb[r][:, m, :], MULT)
 
         combine(0, 0)
-        w2q = quantize(w2g, N, "w2q", 2)
-        combine(1, 0)
-        sigs = sigmoids([first_layer("bank_a", (q0, q1), xq, g) for g in range(4)])
-        q0 = quantize(g0, H, "wq", 10)
-        g1 = group_w13(r3[1], "V")
         combine(0, 1)
-        q1 = quantize(g1, H, "wq", 10)
+        stage_w13(half(stage_w3, 0), raw_w3[0], SCALAR_SETS_SHARED["w3"][0])
+        combine(1, 0)
+        stage_w13(half(stage_w3, 1), raw_w3[1], SCALAR_SETS_SHARED["w3"][1])
+        stage_second(raw_w2, SCALAR_SETS_SHARED["w2"])
+        sigmoids = [raw_w3[1][:, g, :] for g in range(4)]
+        for g in range(4):
+            first_layer(banks_a[g], w1q, tokens, g)
+            sigmoid_of(banks_a[g], sigmoids[g])
+        w3q = [quantize_w13(stage_w3, 0)]
         combine(1, 1)
-        both = keep.tile([P, 2, T], F32, name="both")
-        nc.vector.tensor_tensor(both[:], routed[0][:], routed[1][:], add)
-        for half in range(2):
-            h = pool.tile([P, C, PACK], BF16, name="h", bufs=3, align_bytes=64)
-            mults(h, [first_layer("bank_b", (q0, q1), xq, 2 * half + g) for g in range(2)], sigs[2 * half : 2 * half + 2])
-            hq = quantize_h(h)
-            y = second_layer(w2q, hq)
-            tokens = slice(half * C, (half + 1) * C)
+        w3q.append(quantize_w13(stage_w3, 1))
+        w2q = quantize_w2()
+
+        routed_sum = keep.tile([P, 2, T], F32, name="routed_sum")
+        halves = [slice(k * C, (k + 1) * C) for k in range(2)]
+        for cols in halves:
+            nc.gpsimd.tensor_tensor(routed_sum[:, :, cols], routed[0][:, :, cols], routed[1][:, :, cols], ADD)
+
+        for k, cols in enumerate(halves):
+            groups = (2 * k, 2 * k + 1)
+            for g in groups:
+                first_layer(banks_b[g], w3q, tokens, g)
+            h = hidden([banks_b[g] for g in groups], [sigmoids[g] for g in groups])
+            y = second_layer(banks_a[k], w2q, quantize_hidden(h))
             result = pool.tile([P, 2, C], F32, name="result", bufs=2)
-            nc.vector.tensor_tensor(result[:], y[:], both[:, :, tokens], add)
-            nc.sync.dma_start(out[:, tokens].rearrange("(m p) t -> p m t", p=P), result[:])
+            nc.vector.tensor_tensor(result[:], y, routed_sum[:, :, cols], ADD)
+            nc.sync.dma_start(out[:, cols].rearrange("(m p) t -> p m t", p=P), result[:])

from contextlib import ExitStack

import concourse.mybir as mybir

FLOPS = 3623878656

K, T, E, C, H, N = 1024, 512, 4, 256, 512, 256
P = 128
PACK = 4
K_PASS = P * PACK
PASSES = K // K_PASS
GROUP = 128
LINE = 16

SCALAR_SETS = {"w1": (128, 96), "w3": (0, 128), "w2": 32}
SCALAR_SETS_SHARED = {"w1": (128, 96), "w3": (96, 128), "w2": 64}

F32 = mybir.dt.float32
BF16 = mybir.dt.bfloat16
I32 = mybir.dt.int32
U32 = mybir.dt.uint32
U16 = mybir.dt.uint16
U8 = mybir.dt.uint8
FP8X4 = mybir.dt.float8_e4m3fn_x4
MULT = mybir.AluOpType.mult
ADD = mybir.AluOpType.add
SIGMOID = mybir.ActivationFunctionType.Sigmoid


def tile_moe_shr_glu_sigmoid_kernel(
    tc, xT, w1, w3, w2, gate, offs, pos1, pos2, out
):
    nc = tc.nc
    with ExitStack() as ctx:
        keep = ctx.enter_context(tc.tile_pool(name="keep", bufs=1))
        pool = ctx.enter_context(tc.tile_pool(name="pool", bufs=1))
        psum = ctx.enter_context(tc.psum_pool(name="psum", bufs=1))

        offs_sb = keep.tile([P, E * C // LINE], U16, name="offs_sb")
        pos_sb = [keep.tile([P, T // LINE], U16, name="pos_sb%d" % r) for r in range(2)]
        gate_sb = [keep.tile([P, 2, T], F32, name="gate_sb%d" % r) for r in range(2)]

        warm = keep.tile([P, 1], F32, name="warm")
        nc.vector.memset(warm[:], 0.0)
        nc.scalar.activation(warm[:], warm[:], SIGMOID)

        stages_w1 = [keep.tile([P, PASSES * H * PACK], BF16, name="stage_w1_%d" % i, align_bytes=64) for i in range(2)]
        stage_w3 = keep.tile([P, PASSES * H * PACK], BF16, name="stage_w3", align_bytes=64)
        stage_w2 = keep.tile([P, N * PACK], BF16, name="stage_w2", align_bytes=64)

        banks_a = [psum.tile([P, PACK, GROUP], F32, name="bank_a%d" % i) for i in range(4)]
        banks_b = [psum.tile([P, PACK, GROUP], F32, name="bank_b%d" % i) for i in range(4)]

        y_slots = [keep.tile([P, E * C], F32, name="y_slots%d" % m) for m in range(2)]


        def four_rows(rows):
            return rows.rearrange("(p j) w -> p j w", j=PACK)

        def load_pass(rows):
            raw = pool.tile([P, PACK, H], F32, name="raw", bufs=9)
            nc.sync.dma_start(raw[:], four_rows(rows))
            return raw

        def load_w13(w, e, c):
            return load_pass(w[e][c * K_PASS : (c + 1) * K_PASS, :])

        def load_w2(e):
            raw_w2 = pool.tile([P, PACK, N], F32, name="raw_w2", bufs=2)
            nc.sync.dma_start(raw_w2[:], four_rows(w2[e]))
            return raw_w2

        def load_expert(e):
            raw_w1 = [load_w13(w1, e, c) for c in range(PASSES)]
            raw_w3 = [load_w13(w3, e, c) for c in range(PASSES)]
            return raw_w1, raw_w3, load_w2(e)

        def load_gate(r):
            nc.sync.dma_start(gate_sb[r][:], gate[r].rearrange("(m p) t -> p m t", p=P))

        def load_shared_expert():
            raw_w1 = [load_w13(w1, E, c) for c in range(PASSES)]
            nc.sync.dma_start(pos_sb[0][:], pos1)
            nc.sync.dma_start(pos_sb[1][:], pos2)
            load_gate(0)
            raw_w3 = [load_w13(w3, E, c) for c in range(PASSES)]
            raw_w2 = load_w2(E)
            load_gate(1)
            return raw_w1, raw_w3, raw_w2


        def copy(engine, dst, src):
            if engine == "scalar":
                nc.scalar.copy(dst, src)
            else:
                nc.vector.tensor_copy(dst, src)

        def split_copy(dst, src, scalar_sets, sets):
            for engine, lo, hi in (("scalar", 0, scalar_sets), ("vector", scalar_sets, sets)):
                if lo < hi:
                    copy(engine, dst[:, lo:hi], src[:, lo:hi])

        def half(stage, c):
            return stage[:, c * H * PACK : (c + 1) * H * PACK]

        def stage_w13(dst, raw, scalar_sets):
            split_copy(
                dst.rearrange("p (t m j) -> p m j t", t=PACK, j=PACK),
                raw[:].rearrange("p j (m t) -> p m j t", t=PACK),
                scalar_sets,
                H // PACK,
            )

        def stage_second(raw_w2, scalar_sets):
            split_copy(
                stage_w2[:].rearrange("p (m i j) -> p m j i", i=4, j=PACK),
                raw_w2[:].rearrange("p j (m i) -> p m j i", i=4),
                scalar_sets,
                N // 4,
            )

        def quantize(staged, width, name, bufs):
            codes = pool.tile([P, width], U32, name=name + "_codes", bufs=bufs, align_bytes=64)
            scales = pool.tile([P, width], U8, name=name + "_scales", bufs=bufs, align_bytes=64)
            nc.vector.quantize_mx(out=codes[:].bitcast(FP8X4), scales=scales[:], in_=staged)
            return codes, scales

        def quantize_w13(stage, c):
            return quantize(half(stage, c), H, "wq", 8)

        def quantize_w2():
            return quantize(stage_w2[:], N, "w2q", 3)

        def by_pass(operand, width):
            codes, scales = operand
            return [(codes[:, c * width : (c + 1) * width], scales[:, c * width : (c + 1) * width]) for c in range(PASSES)]


        token_pairs = [keep.tile([P, 2 * T * 2], BF16, name="token_pairs%d" % c, align_bytes=64) for c in range(PASSES)]

        def pair_plane(c, u):
            return token_pairs[c][:, u * 2 * T : (u + 1) * 2 * T]

        def load_tokens(c):
            raw = pool.tile([P, PACK, T], F32, name="raw", bufs=9)
            for u in (1, 0):
                rows = slice(2 * u, 2 * u + 2)
                nc.sync.dma_start(raw[:, rows, :], four_rows(xT[c * K_PASS : (c + 1) * K_PASS, :])[:, rows, :])
            return raw

        def pair_rows(raw, c, u, engine):
            copy(
                engine,
                pair_plane(c, u).rearrange("p (m i e) -> p m e i", i=4, e=2),
                raw[:, 2 * u : 2 * u + 2, :].rearrange("p e (m i) -> p m e i", i=4),
            )

        def stage_tokens(stage, e, c):
            if e < E:
                lists = offs_sb[:, e * C // LINE : (e + 1) * C // LINE]
                words = stage[:, (c + 1) * C * PACK : (c + 2) * C * PACK].bitcast(U32).rearrange("p (s u) -> p s u", u=2)
                for u in (1, 0):
                    nc.vector.tensor_copy(words[:, :, u], pair_plane(c, u).bitcast(U32).indirect(lists))
            else:
                nc.vector.tensor_copy(
                    half(stage, c).bitcast(I32).rearrange("p (s u) -> p s u", u=2),
                    token_pairs[c][:].bitcast(I32).rearrange("p (u s) -> p s u", u=2),
                )

        def quantize_tokens(stage, e):
            if e < E:
                return by_pass(quantize(stage[:, C * PACK : (1 + PASSES) * C * PACK], PASSES * C, "xq", 2), C)
            return by_pass(quantize(stage[:], PASSES * T, "xsq", 1), T)


        def matmul_mx(acc, weights, weight_cols, moving, cols, start, stop):
            nc.tensor.matmul_mx(
                out=acc,
                lhsT=weights[0][:, weight_cols].bitcast(FP8X4),
                lhsT_scale=weights[1][:, weight_cols],
                rhs=moving[0][:, cols].bitcast(FP8X4),
                rhs_scale=moving[1][:, cols],
                start=start,
                stop=stop,
            )

        def first_layer(bank, weights, tokens, g):
            cols = slice(g * GROUP, (g + 1) * GROUP)
            for t in range(PACK):
                for c in range(PASSES):
                    matmul_mx(
                        bank[:, t, :], weights[c], slice(t * P, (t + 1) * P), tokens[c], cols, c == 0, c == PASSES - 1
                    )

        def sigmoid_of(bank, dst):
            nc.scalar.activation(dst.rearrange("p (s t) -> p s t", t=PACK), bank[:].rearrange("p t s -> p s t"), SIGMOID)

        def hidden(banks, sigmoids):
            h = pool.tile([P, C, PACK], BF16, name="h", bufs=2, align_bytes=64)
            for g in range(2):
                nc.vector.tensor_tensor(
                    h[:, g * GROUP : (g + 1) * GROUP, :],
                    banks[g][:].rearrange("p t s -> p s t"),
                    sigmoids[g].rearrange("p (s t) -> p s t", t=PACK),
                    MULT,
                )
            return h

        def quantize_hidden(h):
            return quantize(h[:].rearrange("p s t -> p (s t)"), C, "hq", 3)

        def second_layer(bank, weights, h):
            y = bank[:].rearrange("p t s -> p (t s)").rearrange("p (m s) -> p m s", m=2)
            for m in range(2):
                matmul_mx(y[:, m, :], weights, slice(m * P, (m + 1) * P), h, slice(0, C), True, True)
            return y

        def keep_results(y, e, engine):
            for m in range(2):
                copy(engine, y_slots[m][:, e * C : (e + 1) * C], y[:, m, :])


        nc.sync.dma_start(offs_sb[:], offs)
        raw_tokens = [load_tokens(c) for c in range(PASSES)]
        for c in range(PASSES):
            for u in (1, 0):
                pair_rows(raw_tokens[c], c, u, "scalar" if (c, u) == (1, 1) else "vector")

        raws = load_expert(0)
        for c in range(PASSES):
            stage_tokens(stages_w1[1], 0, c)
        tokens = quantize_tokens(stages_w1[1], 0)

        for e in range(E):
            raw_w1, raw_w3, raw_w2 = raws
            stage = stages_w1[e % 2]
            stage_w13(half(stage, 0), raw_w1[0], SCALAR_SETS["w1"][0])
            raws = load_expert(e + 1) if e + 1 < E else load_shared_expert()
            if e > 0:
                sigmoids = [raw_w1[0][:, g, :] for g in range(2)]
                for g in range(2):
                    sigmoid_of(a[g], sigmoids[g])
                if e > 1:
                    keep_results(second_layer(a[0], w2q, hq), e - 2, "scalar")
                h = hidden(b, sigmoids)
                w2q = quantize_w2()
                hq = quantize_hidden(h)
            w1q = [quantize_w13(stage, 0)]
            stage_tokens(stage, e + 1, 0)
            stage_w13(half(stage, 1), raw_w1[1], SCALAR_SETS["w1"][1])
            w1q.append(quantize_w13(stage, 1))
            stage_tokens(stage, e + 1, 1)
            a = banks_a[2 * (e % 2) : 2 * (e % 2) + 2]
            b = banks_b[2 * (e % 2) : 2 * (e % 2) + 2]
            for g in range(2):
                first_layer(a[g], w1q, tokens, g)
            for c in range(PASSES):
                stage_w13(half(stage_w3, c), raw_w3[c], SCALAR_SETS["w3"][c])
            w3q = [quantize_w13(stage_w3, 0)]
            next_tokens = quantize_tokens(stage, e + 1)
            w3q.append(quantize_w13(stage_w3, 1))
            for g in range(2):
                first_layer(b[g], w3q, tokens, g)
            stage_second(raw_w2, SCALAR_SETS["w2"])
            tokens = next_tokens


        raw_w1, raw_w3, raw_w2 = raws
        stage = stages_w1[E % 2]
        stage_w13(half(stage, 0), raw_w1[0], SCALAR_SETS_SHARED["w1"][0])
        sigmoids = [raw_w1[0][:, g, :] for g in range(2)]
        for g in range(2):
            sigmoid_of(a[g], sigmoids[g])
        keep_results(second_layer(a[0], w2q, hq), E - 2, "scalar")
        h = hidden(b, sigmoids)
        w2q = quantize_w2()
        hq = quantize_hidden(h)
        y = second_layer(banks_b[0], w2q, hq)
        stage_w13(half(stage, 1), raw_w1[1], SCALAR_SETS_SHARED["w1"][1])
        w1q = [quantize_w13(stage, 0)]
        keep_results(y, E - 1, "vector")
        w1q.append(quantize_w13(stage, 1))


        routed = [keep.tile([P, 2, T], F32, name="routed%d" % r) for r in range(2)]

        def combine(r, m):
            nc.vector.tensor_tensor(routed[r][:, m, :], y_slots[m][:].indirect(pos_sb[r][:]), gate_sb[r][:, m, :], MULT)

        combine(0, 0)
        combine(0, 1)
        stage_w13(half(stage_w3, 0), raw_w3[0], SCALAR_SETS_SHARED["w3"][0])
        combine(1, 0)
        stage_w13(half(stage_w3, 1), raw_w3[1], SCALAR_SETS_SHARED["w3"][1])
        stage_second(raw_w2, SCALAR_SETS_SHARED["w2"])
        sigmoids = [raw_w3[1][:, g, :] for g in range(4)]
        for g in range(4):
            first_layer(banks_a[g], w1q, tokens, g)
            sigmoid_of(banks_a[g], sigmoids[g])
        w3q = [quantize_w13(stage_w3, 0)]
        combine(1, 1)
        w3q.append(quantize_w13(stage_w3, 1))
        w2q = quantize_w2()

        routed_sum = keep.tile([P, 2, T], F32, name="routed_sum")
        halves = [slice(k * C, (k + 1) * C) for k in range(2)]
        for cols in halves:
            nc.gpsimd.tensor_tensor(routed_sum[:, :, cols], routed[0][:, :, cols], routed[1][:, :, cols], ADD)

        for k, cols in enumerate(halves):
            groups = (2 * k, 2 * k + 1)
            for g in groups:
                first_layer(banks_b[g], w3q, tokens, g)
            h = hidden([banks_b[g] for g in groups], [sigmoids[g] for g in groups])
            y = second_layer(banks_a[k], w2q, quantize_hidden(h))
            result = pool.tile([P, 2, C], F32, name="result", bufs=2)
            nc.vector.tensor_tensor(result[:], y, routed_sum[:, :, cols], ADD)
            nc.sync.dma_start(out[:, cols].rearrange("(m p) t -> p m t", p=P), result[:])
